import numpy as np
import ml_dtypes


def mxq(x, axis, fmt="e4m3"):
    dtype, down = {"e4m3": (ml_dtypes.float8_e4m3fn, 7), "e5m2": (ml_dtypes.float8_e5m2, 14)}[fmt]
    v = np.moveaxis(np.asarray(x, np.float32).astype(ml_dtypes.bfloat16).astype(np.float64), axis, -1)
    blocks = v.reshape(v.shape[:-1] + (-1, 32))
    amax = np.abs(blocks).max(-1, keepdims=True)
    byte = np.maximum(np.where(amax > 0, np.frexp(amax)[1] - 1 + 127, 0) - down, 1)
    scale = np.exp2(byte - 127.0)
    codes = (blocks / scale).astype(np.float32).astype(dtype).astype(np.float64)
    return np.moveaxis((codes * scale).reshape(v.shape), -1, axis)


WIDE = False


def mx_kscale(k):
    if not WIDE:
        return np.ones(k)
    levels = np.array([10, -10, 5, -5, 0])
    if k % 512:
        return np.exp2(np.random.permutation(np.resize(levels, k // 32))).repeat(32)
    a = np.empty((k // 512, 16))
    for p in range(k // 512):
        a[p, :8] = np.random.permutation(np.resize(levels, 8))
        for g in range(8):
            far = levels[np.abs(levels - a[p, g]) >= 10]
            a[p, g + 8] = far[np.random.randint(len(far))]
    return np.exp2(a.ravel()).repeat(32)


def f64(x):
    return np.asarray(x).astype(np.float64)


def striped(idx):
    return np.tile(np.asarray(idx).reshape(-1, 16).T, (8, 1)).astype(np.uint16)


def unstriped(offs):
    return offs[:16].T.reshape(-1).astype(np.int64)


E2M1 = np.array([0.0, 0.5, 1.0, 1.5, 2.0, 3.0, 4.0, 6.0, -0.0, -0.5, -1.0, -1.5, -2.0, -3.0, -4.0, -6.0])


def pack_weight(w, fmt):
    k, n = w.shape
    w = f64(np.asarray(w, np.float32).astype(ml_dtypes.bfloat16)).reshape(k // 32, 32, n)
    amax = np.abs(w).max(1)
    if fmt == "e4m3":
        byte = np.frexp(amax)[1] - 1 + 127 - 7
    else:
        mant, ex = np.frexp(amax / 6.0)
        byte = np.where(mant > 0.5, ex, ex - 1) + 127
    byte = np.clip(np.where(amax > 0, byte, 1), 1, 254)
    scaled = (w * np.exp2(127.0 - byte)[:, None, :]).reshape(k, n).astype(np.float32)
    by_word = np.ascontiguousarray(scaled.reshape(k // 512, 128, 4, n).transpose(0, 1, 3, 2))
    if fmt == "e4m3":
        words = by_word.astype(ml_dtypes.float8_e4m3fn).view(np.uint8)
    else:
        c = by_word.astype(ml_dtypes.float4_e2m1fn).view(np.uint8) & 0xF
        words = (c[..., 0::2] | (c[..., 1::2] << 4)).reshape(k // 512, 128, 2 * n)
    return np.ascontiguousarray(words), np.ascontiguousarray(byte.astype(np.uint8).reshape(k // 512, 16, n))


def unpack_weight(words, scales, fmt):
    g, _, n = scales.shape
    words = np.ascontiguousarray(words).reshape(g, 128, n, -1)
    if fmt == "e4m3":
        vals = words.view(ml_dtypes.float8_e4m3fn).astype(np.float64)
    else:
        nib = np.empty((g, 128, n, 4), np.uint8)
        nib[..., 0::2] = words & 0xF
        nib[..., 1::2] = words >> 4
        vals = E2M1[nib]
    vals = vals * np.repeat(np.exp2(scales.astype(np.float64) - 127.0), 8, axis=1)[..., None]
    return vals.transpose(0, 1, 3, 2).reshape(g * 512, n)


def softplus(v):
    return np.log(1.0 + np.exp(v))


K, T, J, I, N = 512, 1024, 512, 512, 256


def setup_inputs():
    n = np.random.standard_normal
    idx = np.random.permutation(T)[:J]
    idx2 = np.random.permutation(T)[:I]
    fk = mx_kscale(K)
    xtp = pack_weight(n((K, T)) / fk[:, None], "e4m3")
    wap = pack_weight(n((K, N)) * 1 / np.sqrt(K) * fk[:, None], "e2m1")
    wbp = pack_weight(n((K, N)) * 1 / np.sqrt(K) * fk[:, None], "e2m1")
    vbp = pack_weight(n((K, N)) * 1 / np.sqrt(K) * fk[:, None], "e4m3")
    return {
        "xt_words": xtp[0],
        "xt_scales": xtp[1],
        "wa_words": wap[0],
        "wa_scales": wap[1],
        "va": (n((K, N)) * 1 / np.sqrt(K) * fk[:, None]).astype(np.float32),
        "wb_words": wbp[0],
        "wb_scales": wbp[1],
        "vb_words": vbp[0],
        "vb_scales": vbp[1],
        "pr": (np.random.uniform(0.4, 2.0, (N, T))).astype(np.float32),
        "old": (1.0 * n((N, T))).astype(np.float32),
        "offs": striped(idx),
        "offs2": striped(idx2),
    }


def reference(xt_words, xt_scales, wa_words, wa_scales, va, wb_words, wb_scales, vb_words, vb_scales, pr, old, offs, offs2):
    idx = unstriped(offs)
    idx2 = unstriped(offs2)
    xtu = unpack_weight(xt_words, xt_scales, "e4m3")
    wau = unpack_weight(wa_words, wa_scales, "e2m1")
    wbu = unpack_weight(wb_words, wb_scales, "e2m1")
    vbu = unpack_weight(vb_words, vb_scales, "e4m3")
    xtidxg = xtu[:, idx]
    a = wau.T @ xtidxg
    vaq = mxq(f64(va), 0, "e4m3")
    u = vaq.T @ xtidxg
    xtidx2g = xtu[:, idx2]
    b = wbu.T @ xtidx2g
    v = vbu.T @ xtidx2g
    sa = softplus(u)
    sb = softplus(v)
    pa = sa * a
    pb = sb * b
    na = np.zeros((N, T))
    na[:, idx] = pa
    da = np.zeros((N, T))
    da[:, idx] = sa
    nb = np.zeros((N, T))
    nb[:, idx2] = pb
    db = np.zeros((N, T))
    db[:, idx2] = sb
    y = (na + nb + f64(pr) * f64(old)) / (da + db + f64(pr))
    return y

@@ -1,0 +1,227 @@
+from contextlib import ExitStack
+
+import concourse.mybir as mybir
+from concourse.masks import make_identity
+
+K, T, J, N = 512, 1024, 512, 256
+FLOPS = 4 * 2 * K * N * J
+
+F32 = mybir.dt.float32
+BF16 = mybir.dt.bfloat16
+I32 = mybir.dt.int32
+U32 = mybir.dt.uint32
+U16 = mybir.dt.uint16
+U8 = mybir.dt.uint8
+FP8X4 = mybir.dt.float8_e4m3fn_x4
+FP4X4 = mybir.dt.float4_e2m1fn_x4
+ACT = mybir.ActivationFunctionType
+ALU = mybir.AluOpType
+
+P = 128
+BANK = 512
+TINY = 2.0 ** -60
+
+
+def tile_moe_experts_write_with_weights_kernel(
+    tc, xt_words, xt_scales, wa_words, wa_scales, va, wb_words, wb_scales, vb_words, vb_scales, pr, old, offs, offs2, out
+):
+    nc = tc.nc
+    with ExitStack() as ctx:
+        lists = ctx.enter_context(tc.tile_pool(name="lists", bufs=1))
+        sb = ctx.enter_context(tc.tile_pool(name="sb", bufs=1))
+        psum = ctx.enter_context(tc.psum_pool(name="psum", bufs=1))
+
+        def tile(name, shape, dtype):
+            return sb.tile(shape, dtype, name=name, align_bytes=64)
+
+        banks = [psum.tile([P, BANK], F32, name="bank%d" % i) for i in range(8)]
+
+        list_a = lists.tile([P, J // 16], U16, name="list_a")
+        list_b = lists.tile([P, J // 16], U16, name="list_b")
+        x_words = tile("x_words", [P, T], I32)
+        x_plane = tile("x_plane", [P, T], U8)
+        w_planes = tile("w_planes", [P, 3 * N], U8)
+        wa_plane, vb_plane, wb_plane = (w_planes[:, i * N : (i + 1) * N] for i in range(3))
+        wa_t = tile("wa_t", [P, 2 * N], U8)
+        wb_t = tile("wb_t", [P, 2 * N], U8)
+        vb_t = tile("vb_t", [P, N], I32)
+        va_raw = [tile("va_raw%d" % r, [P, 4, P], F32) for r in range(2)]
+        pr_t = [tile("pr%d" % r, [P, T], F32) for r in range(2)]
+        old_t = [tile("old%d" % r, [P, T], F32) for r in range(2)]
+        win = {name: tile("win_" + name, [P, T], F32) for name in ("a1", "a2", "b1", "b2")}
+        tiny = tile("tiny", [P, 1], F32)
+        ident = tile("ident", [P, P], F32)
+
+        def load_plane(queue, plane, scales):
+            for s in range(4):
+                queue.dma_start(out=plane[s:P:32, :].bitcast(I32), in_=scales[0][s:16:4, :].bitcast(I32))
+
+        nc.gpsimd.memset(x_plane[:].bitcast(I32), 0)
+        nc.gpsimd.memset(w_planes[:].bitcast(I32), 0)
+        nc.gpsimd.memset(tiny[:], TINY)
+        for name in ("a1", "a2", "b1", "b2"):
+            nc.vector.memset(win[name][:], 0.0)
+        make_identity(nc, ident[:])
+
+        va_rows = va.rearrange("(p j) n -> p j n", j=4)
+        nc.sync.dma_start(list_a[:], offs)
+        nc.sync.dma_start(out=va_raw[0][:], in_=va_rows[:, :, 0:P])
+        load_plane(nc.sync, x_plane, xt_scales)
+        nc.sync.dma_start(out=x_words[:], in_=xt_words[0].rearrange("p n t -> p (n t)").bitcast(I32))
+        nc.sync.dma_start(list_b[:], offs2)
+        nc.sync.dma_start(out=wa_t[:].bitcast(I32), in_=wa_words[0].bitcast(I32))
+        nc.sync.dma_start(out=va_raw[1][:], in_=va_rows[:, :, P : 2 * P])
+        nc.sync.dma_start(out=pr_t[0][:], in_=pr[0:P, :])
+        nc.sync.dma_start(out=old_t[0][:], in_=old[0:P, :])
+        load_plane(nc.sync, wa_plane, wa_scales)
+        nc.sync.dma_start(out=pr_t[1][:], in_=pr[P : 2 * P, :])
+        nc.sync.dma_start(out=old_t[1][:], in_=old[P : 2 * P, :])
+        nc.sync.dma_start(out=vb_t[:], in_=vb_words[0].rearrange("p n t -> p (n t)").bitcast(I32))
+        load_plane(nc.sync, vb_plane, vb_scales)
+        nc.sync.dma_start(out=wb_t[:].bitcast(I32), in_=wb_words[0].bitcast(I32))
+        load_plane(nc.sync, wb_plane, wb_scales)
+
+        va_codes = [tile("va_codes%d" % r, [P, P], U32) for r in range(2)]
+        va_plane = [tile("va_plane%d" % r, [P, P], U8) for r in range(2)]
+
+        def quantise_va(r):
+            grouped = tile("va_bf%d" % r, [P, P, 4], BF16)
+            nc.vector.tensor_copy(
+                out=grouped[:].rearrange("p (c i) t -> p c t i", i=4),
+                in_=va_raw[r][:].rearrange("p t (c i) -> p c t i", i=4),
+            )
+            nc.vector.quantize_mx(
+                out=va_codes[r][:].bitcast(FP8X4), scales=va_plane[r][:], in_=grouped[:].rearrange("p n t -> p (n t)")
+            )
+
+        def gather_tokens(name, lst):
+            words = tile("g_words_" + name, [P, J], U32)
+            plane = tile("g_plane_" + name, [P, J], U8)
+            nc.vector.tensor_copy(words[:], x_words[:].bitcast(U32).indirect(lst[:]))
+            nc.vector.tensor_copy(plane[:], x_plane[:].indirect(lst[:]))
+            return words, plane
+
+        def product(bank, lhs, lhs_plane, tokens):
+            nc.tensor.matmul_mx(
+                out=bank[:], lhsT=lhs, lhsT_scale=lhs_plane, rhs=tokens[0][:].bitcast(FP8X4), rhs_scale=tokens[1][:],
+                start=True, stop=True,
+            )
+
+        def cols(r):
+            return slice(r * P, (r + 1) * P)
+
+        def fp4_cols(words, r):
+            return words[:, 2 * r * P : 2 * (r + 1) * P].bitcast(FP4X4)
+
+        keys = ("a0", "b0", "b1", "a1")
+        pair = {key: tile("pair_" + key, [P, 2 * J], F32) for key in keys}
+        wgt = {key: pair[key][:, 0:J] for key in keys}
+        val = {key: pair[key][:, J : 2 * J] for key in keys}
+        lg = {key: tile("lg_" + key, [P, J], F32) for key in keys}
+        lists_of = {"a": list_a, "b": list_b}
+
+        def sigmoid(key, bank):
+            nc.scalar.activation(val[key], bank[:], ACT.Sigmoid, scale=-1.0)
+
+        def logarithm(key):
+            nc.scalar.activation(lg[key][:], val[key], ACT.Ln, bias=tiny[:])
+
+        def softplus(key, bank):
+            nc.vector.scalar_tensor_tensor(wgt[key], lg[key][:], -1.0, bank[:], ALU.mult, ALU.max)
+
+        def values(key, bank):
+            nc.scalar.copy(val[key], bank[:])
+
+        def scatter_weights(key, window):
+            nc.vector.tensor_copy(win[window][:].indirect(lists_of[key[0]][:]), wgt[key])
+
+        def scatter_products(key, window):
+            nc.vector.tensor_tensor(win[window][:].indirect(lists_of[key[0]][:]), wgt[key], val[key], ALU.mult)
+
+        def turn_add(two_banks, src, first, last):
+            for h in range(2):
+                for c in range(4):
+                    nc.tensor.matmul(
+                        two_banks[h][:, cols(c)], lhsT=src[:, cols(4 * h + c)], rhs=ident[:], is_transpose=True,
+                        start=(first and c == 0), stop=(last and c == 3),
+                    )
+
+        def turn_back(name, two_banks, func):
+            for h in range(2):
+                mid = tile("mid_%s%d" % (name, h), [P, BANK], F32)
+                nc.scalar.activation(mid[:], two_banks[h][:], func)
+                for c in range(4):
+                    nc.tensor.transpose(two_banks[h][:, cols(c)], mid[:, cols(c)], ident[:])
+
+        def half(h):
+            return slice(h * BANK, (h + 1) * BANK)
+
+        quantise_va(0)
+        tok_a = gather_tokens("a", list_a)
+        product(banks[0], va_codes[0][:].bitcast(FP8X4), va_plane[0][:], tok_a)
+        sigmoid("a0", banks[0])
+        logarithm("a0")
+        product(banks[1], fp4_cols(wa_t, 0), wa_plane[:, cols(0)], tok_a)
+        values("a0", banks[1])
+        tok_b = gather_tokens("b", list_b)
+        quantise_va(1)
+        po0 = tile("po0", [P, T], F32)
+        nc.vector.tensor_tensor(po0[:], pr_t[0][:], old_t[0][:], ALU.mult)
+        softplus("a0", banks[0])
+        scatter_weights("a0", "a1")
+        scatter_products("a0", "a2")
+
+        product(banks[0], va_codes[1][:].bitcast(FP8X4), va_plane[1][:], tok_a)
+        product(banks[1], vb_t[:, cols(0)].bitcast(FP8X4), vb_plane[:, cols(0)], tok_b)
+        product(banks[3], vb_t[:, cols(1)].bitcast(FP8X4), vb_plane[:, cols(1)], tok_b)
+        product(banks[6], fp4_cols(wa_t, 1), wa_plane[:, cols(1)], tok_a)
+        product(banks[5], fp4_cols(wb_t, 0), wb_plane[:, cols(0)], tok_b)
+        product(banks[7], fp4_cols(wb_t, 1), wb_plane[:, cols(1)], tok_b)
+        for key, b in (("a1", 0), ("b0", 1), ("b1", 3)):
+            sigmoid(key, banks[b])
+        for key in ("a1", "b0", "b1"):
+            logarithm(key)
+        for key, b in (("a1", 6), ("b0", 5), ("b1", 7)):
+            values(key, banks[b])
+        den = [[banks[2], banks[4]], banks[0:2]]
+        num = [[banks[5], banks[3]], banks[6:8]]
+        po1 = pair["a0"]
+        nc.vector.tensor_tensor(po1[:], pr_t[1][:], old_t[1][:], ALU.mult)
+        turn_add(den[0], pr_t[0], True, False)
+        turn_add(den[0], win["a1"], False, False)
+        softplus("a1", banks[0])
+        scatter_weights("a1", "a1")
+        softplus("b0", banks[1])
+        scatter_weights("b0", "b1")
+        softplus("b1", banks[3])
+        scatter_weights("b1", "b2")
+        turn_add(num[0], po0, True, False)
+        turn_add(num[0], win["a2"], False, False)
+        turn_add(den[0], win["b1"], False, True)
+        turn_add(den[1], pr_t[1], True, False)
+        turn_add(den[1], win["a1"], False, False)
+        scatter_products("a1", "a2")
+        turn_add(den[1], win["b2"], False, True)
+        rec = [tile("rec%d" % r, [P, T], F32) for r in range(2)]
+        turn_back("den0", den[0], ACT.Ln)
+        turn_back("den1", den[1], ACT.Ln)
+        for r in range(2):
+            for h in range(2):
+                nc.scalar.activation(rec[r][:, half(h)], den[r][h][:], ACT.Exp, scale=-1.0)
+        scatter_products("b0", "b1")
+        turn_add(num[1], po1, True, False)
+        turn_add(num[1], win["a2"], False, True)
+        turn_back("num1", num[1], ACT.Copy)
+        scatter_products("b1", "b2")
+        turn_add(num[0], win["b1"], False, True)
+        turn_back("num0", num[0], ACT.Copy)
+        y = [tile("y%d" % r, [P, T], F32) for r in range(2)]
+        total = tile("total", [P, T], F32)
+        for h in range(2):
+            nc.vector.tensor_tensor(total[:, half(h)], num[1][h][:], win["b2"][:, half(h)], ALU.add)
+        for h in range(2):
+            nc.vector.tensor_tensor(y[0][:, half(h)], num[0][h][:], rec[0][:, half(h)], ALU.mult)
+            nc.sync.dma_start(out=out[0:P, half(h)], in_=y[0][:, half(h)])
+        for h in range(2):
+            nc.vector.tensor_tensor(y[1][:, half(h)], total[:, half(h)], rec[1][:, half(h)], ALU.mult)
+            nc.sync.dma_start(out=out[P : 2 * P, half(h)], in_=y[1][:, half(h)])

@@ -31,8 +31,8 @@ def tile_moe_experts_write_with_weights_kernel(
         sb = ctx.enter_context(tc.tile_pool(name="sb", bufs=1))
         psum = ctx.enter_context(tc.psum_pool(name="psum", bufs=1))
 
-        def tile(name, shape, dtype):
-            return sb.tile(shape, dtype, name=name, align_bytes=64)
+        def tile(name, shape, dtype, tag=None):
+            return sb.tile(shape, dtype, name=name, tag=tag or name, align_bytes=64)
 
         banks = [psum.tile([P, BANK], F32, name="bank%d" % i) for i in range(8)]
 
@@ -48,7 +48,7 @@ def tile_moe_experts_write_with_weights_kernel(
         va_raw = [tile("va_raw%d" % r, [P, 4, P], F32) for r in range(2)]
         pr_t = [tile("pr%d" % r, [P, T], F32) for r in range(2)]
         old_t = [tile("old%d" % r, [P, T], F32) for r in range(2)]
-        win = {name: tile("win_" + name, [P, T], F32) for name in ("a1", "a2", "b1", "b2")}
+        win = {name: tile("win_" + name, [P, T], F32) for name in ("a1", "a2")}
         tiny = tile("tiny", [P, 1], F32)
         ident = tile("ident", [P, P], F32)
 
@@ -59,7 +59,7 @@ def tile_moe_experts_write_with_weights_kernel(
         nc.gpsimd.memset(x_plane[:].bitcast(I32), 0)
         nc.gpsimd.memset(w_planes[:].bitcast(I32), 0)
         nc.gpsimd.memset(tiny[:], TINY)
-        for name in ("a1", "a2", "b1", "b2"):
+        for name in ("a1", "a2"):
             nc.vector.memset(win[name][:], 0.0)
         make_identity(nc, ident[:])
 
@@ -68,17 +68,17 @@ def tile_moe_experts_write_with_weights_kernel(
         nc.sync.dma_start(out=va_raw[0][:], in_=va_rows[:, :, 0:P])
         load_plane(nc.sync, x_plane, xt_scales)
         nc.sync.dma_start(out=x_words[:], in_=xt_words[0].rearrange("p n t -> p (n t)").bitcast(I32))
-        nc.sync.dma_start(list_b[:], offs2)
         nc.sync.dma_start(out=wa_t[:].bitcast(I32), in_=wa_words[0].bitcast(I32))
+        nc.sync.dma_start(out=vb_t[:], in_=vb_words[0].rearrange("p n t -> p (n t)").bitcast(I32))
+        nc.sync.dma_start(out=wb_t[:].bitcast(I32), in_=wb_words[0].bitcast(I32))
+        nc.sync.dma_start(list_b[:], offs2)
         nc.sync.dma_start(out=va_raw[1][:], in_=va_rows[:, :, P : 2 * P])
+        load_plane(nc.sync, wa_plane, wa_scales)
         nc.sync.dma_start(out=pr_t[0][:], in_=pr[0:P, :])
         nc.sync.dma_start(out=old_t[0][:], in_=old[0:P, :])
-        load_plane(nc.sync, wa_plane, wa_scales)
         nc.sync.dma_start(out=pr_t[1][:], in_=pr[P : 2 * P, :])
         nc.sync.dma_start(out=old_t[1][:], in_=old[P : 2 * P, :])
-        nc.sync.dma_start(out=vb_t[:], in_=vb_words[0].rearrange("p n t -> p (n t)").bitcast(I32))
         load_plane(nc.sync, vb_plane, vb_scales)
-        nc.sync.dma_start(out=wb_t[:].bitcast(I32), in_=wb_words[0].bitcast(I32))
         load_plane(nc.sync, wb_plane, wb_scales)
 
         va_codes = [tile("va_codes%d" % r, [P, P], U32) for r in range(2)]
@@ -97,8 +97,8 @@ def tile_moe_experts_write_with_weights_kernel(
         def gather_tokens(name, lst):
             words = tile("g_words_" + name, [P, J], U32)
             plane = tile("g_plane_" + name, [P, J], U8)
-            nc.vector.tensor_copy(words[:], x_words[:].bitcast(U32).indirect(lst[:]))
             nc.vector.tensor_copy(plane[:], x_plane[:].indirect(lst[:]))
+            nc.vector.tensor_copy(words[:], x_words[:].bitcast(U32).indirect(lst[:]))
             return words, plane
 
         def product(bank, lhs, lhs_plane, tokens):
@@ -165,63 +165,82 @@ def tile_moe_experts_write_with_weights_kernel(
         values("a0", banks[1])
         tok_b = gather_tokens("b", list_b)
         quantise_va(1)
-        po0 = tile("po0", [P, T], F32)
-        nc.vector.tensor_tensor(po0[:], pr_t[0][:], old_t[0][:], ALU.mult)
+        win["b1"] = tile("win_b1", [P, T], F32, tag="va_bf1")
+        nc.gpsimd.memset(win["b1"][:], 0.0)
         softplus("a0", banks[0])
+        win["b2"] = tile("win_b2", [P, T], F32, tag="lg_a0")
+        nc.gpsimd.memset(win["b2"][:], 0.0)
         scatter_weights("a0", "a1")
         scatter_products("a0", "a2")
 
         product(banks[0], va_codes[1][:].bitcast(FP8X4), va_plane[1][:], tok_a)
-        product(banks[1], vb_t[:, cols(0)].bitcast(FP8X4), vb_plane[:, cols(0)], tok_b)
+        product(banks[6], vb_t[:, cols(0)].bitcast(FP8X4), vb_plane[:, cols(0)], tok_b)
         product(banks[3], vb_t[:, cols(1)].bitcast(FP8X4), vb_plane[:, cols(1)], tok_b)
-        product(banks[6], fp4_cols(wa_t, 1), wa_plane[:, cols(1)], tok_a)
+        product(banks[1], fp4_cols(wa_t, 1), wa_plane[:, cols(1)], tok_a)
         product(banks[5], fp4_cols(wb_t, 0), wb_plane[:, cols(0)], tok_b)
         product(banks[7], fp4_cols(wb_t, 1), wb_plane[:, cols(1)], tok_b)
-        for key, b in (("a1", 0), ("b0", 1), ("b1", 3)):
+        for key, b in (("a1", 0), ("b0", 6), ("b1", 3)):
             sigmoid(key, banks[b])
         for key in ("a1", "b0", "b1"):
             logarithm(key)
-        for key, b in (("a1", 6), ("b0", 5), ("b1", 7)):
+        for key, b in (("b0", 5), ("a1", 1), ("b1", 7)):
             values(key, banks[b])
         den = [[banks[2], banks[4]], banks[0:2]]
         num = [[banks[5], banks[3]], banks[6:8]]
-        po1 = pair["a0"]
-        nc.vector.tensor_tensor(po1[:], pr_t[1][:], old_t[1][:], ALU.mult)
+        po0 = pair["a0"]
+        nc.gpsimd.tensor_tensor(po0[:], pr_t[0][:], old_t[0][:], ALU.mult)
         turn_add(den[0], pr_t[0], True, False)
         turn_add(den[0], win["a1"], False, False)
         softplus("a1", banks[0])
+        po1 = tile("po1", [P, T], F32, tag="lg_a1")
+        nc.gpsimd.tensor_tensor(po1[:], pr_t[1][:], old_t[1][:], ALU.mult)
+        softplus("b0", banks[6])
         scatter_weights("a1", "a1")
-        softplus("b0", banks[1])
-        scatter_weights("b0", "b1")
         softplus("b1", banks[3])
+        scatter_weights("b0", "b1")
         scatter_weights("b1", "b2")
-        turn_add(num[0], po0, True, False)
-        turn_add(num[0], win["a2"], False, False)
-        turn_add(den[0], win["b1"], False, True)
         turn_add(den[1], pr_t[1], True, False)
         turn_add(den[1], win["a1"], False, False)
+        turn_add(num[0], win["a2"], True, False)
+        turn_add(num[0], po0, False, False)
+        turn_add(num[1], po1, True, False)
+        turn_add(den[0], win["b1"], False, True)
+        ln_den0 = tile("ln_den0", [P, T], F32)
+        for h in range(2):
+            nc.scalar.activation(ln_den0[:, half(h)], den[0][h][:], ACT.Ln)
         scatter_products("a1", "a2")
         turn_add(den[1], win["b2"], False, True)
-        rec = [tile("rec%d" % r, [P, T], F32) for r in range(2)]
-        turn_back("den0", den[0], ACT.Ln)
-        turn_back("den1", den[1], ACT.Ln)
-        for r in range(2):
-            for h in range(2):
-                nc.scalar.activation(rec[r][:, half(h)], den[r][h][:], ACT.Exp, scale=-1.0)
+        ln_den1 = tile("ln_den1", [P, T], F32)
+        rec0 = tile("rec0", [P, T], F32)
+        rec1_turned = tile("rec1_turned", [P, T], F32)
+        for h in range(2):
+            nc.scalar.activation(ln_den1[:, half(h)], den[1][h][:], ACT.Ln)
+        for h in range(2):
+            for c in range(4):
+                nc.tensor.transpose(den[1][h][:, cols(c)], ln_den0[:, cols(4 * h + c)], ident[:])
+            nc.scalar.activation(rec0[:, half(h)], den[1][h][:], ACT.Exp, scale=-1.0)
+        for h in range(2):
+            nc.scalar.activation(rec1_turned[:, half(h)], ln_den1[:, half(h)], ACT.Exp, scale=-1.0)
         scatter_products("b0", "b1")
-        turn_add(num[1], po1, True, False)
         turn_add(num[1], win["a2"], False, True)
         turn_back("num1", num[1], ACT.Copy)
         scatter_products("b1", "b2")
         turn_add(num[0], win["b1"], False, True)
         turn_back("num0", num[0], ACT.Copy)
         y = [tile("y%d" % r, [P, T], F32) for r in range(2)]
+        num0 = tile("num0", [P, T], F32)
+        for h in range(2):
+            nc.scalar.copy(num0[:, half(h)], num[0][h][:])
+            nc.gpsimd.tensor_tensor(y[0][:, half(h)], num0[:, half(h)], rec0[:, half(h)], ALU.mult)
+        rec1 = num[0]
+        for h in range(2):
+            for c in range(4):
+                nc.tensor.transpose(rec1[h][:, cols(c)], rec1_turned[:, cols(4 * h + c)], ident[:])
         total = tile("total", [P, T], F32)
         for h in range(2):
             nc.vector.tensor_tensor(total[:, half(h)], num[1][h][:], win["b2"][:, half(h)], ALU.add)
         for h in range(2):
-            nc.vector.tensor_tensor(y[0][:, half(h)], num[0][h][:], rec[0][:, half(h)], ALU.mult)
-            nc.sync.dma_start(out=out[0:P, half(h)], in_=y[0][:, half(h)])
+            nc.vector.tensor_tensor(y[1][:, half(h)], rec1[h][:], total[:, half(h)], ALU.mult)
         for h in range(2):
-            nc.vector.tensor_tensor(y[1][:, half(h)], total[:, half(h)], rec[1][:, half(h)], ALU.mult)
-            nc.sync.dma_start(out=out[P : 2 * P, half(h)], in_=y[1][:, half(h)])
+            for r in range(2):
+                nc.sync.dma_start(out=out[r * P : (r + 1) * P, half(h)], in_=y[r][:, half(h)])

@@ -68,25 +68,25 @@ def tile_moe_experts_write_with_weights_kernel(
         nc.sync.dma_start(out=va_raw[0][:], in_=va_rows[:, :, 0:P])
         load_plane(nc.sync, x_plane, xt_scales)
         nc.sync.dma_start(out=x_words[:], in_=xt_words[0].rearrange("p n t -> p (n t)").bitcast(I32))
-        nc.sync.dma_start(out=wa_t[:].bitcast(I32), in_=wa_words[0].bitcast(I32))
-        nc.sync.dma_start(out=vb_t[:], in_=vb_words[0].rearrange("p n t -> p (n t)").bitcast(I32))
-        nc.sync.dma_start(out=wb_t[:].bitcast(I32), in_=wb_words[0].bitcast(I32))
-        nc.sync.dma_start(list_b[:], offs2)
         nc.sync.dma_start(out=va_raw[1][:], in_=va_rows[:, :, P : 2 * P])
-        load_plane(nc.sync, wa_plane, wa_scales)
+        nc.sync.dma_start(out=wa_t[:].bitcast(I32), in_=wa_words[0].bitcast(I32))
+        nc.sync.dma_start(list_b[:], offs2)
         nc.sync.dma_start(out=pr_t[0][:], in_=pr[0:P, :])
         nc.sync.dma_start(out=old_t[0][:], in_=old[0:P, :])
+        load_plane(nc.sync, wa_plane, wa_scales)
+        nc.sync.dma_start(out=vb_t[:], in_=vb_words[0].rearrange("p n t -> p (n t)").bitcast(I32))
+        load_plane(nc.sync, vb_plane, vb_scales)
+        nc.sync.dma_start(out=wb_t[:].bitcast(I32), in_=wb_words[0].bitcast(I32))
         nc.sync.dma_start(out=pr_t[1][:], in_=pr[P : 2 * P, :])
         nc.sync.dma_start(out=old_t[1][:], in_=old[P : 2 * P, :])
-        load_plane(nc.sync, vb_plane, vb_scales)
         load_plane(nc.sync, wb_plane, wb_scales)
 
         va_codes = [tile("va_codes%d" % r, [P, P], U32) for r in range(2)]
         va_plane = [tile("va_plane%d" % r, [P, P], U8) for r in range(2)]
 
-        def quantise_va(r):
+        def quantise_va(r, cast):
             grouped = tile("va_bf%d" % r, [P, P, 4], BF16)
-            nc.vector.tensor_copy(
+            cast(
                 out=grouped[:].rearrange("p (c i) t -> p c t i", i=4),
                 in_=va_raw[r][:].rearrange("p t (c i) -> p c t i", i=4),
             )
@@ -156,7 +156,7 @@ def tile_moe_experts_write_with_weights_kernel(
         def half(h):
             return slice(h * BANK, (h + 1) * BANK)
 
-        quantise_va(0)
+        quantise_va(0, nc.vector.tensor_copy)
         tok_a = gather_tokens("a", list_a)
         product(banks[0], va_codes[0][:].bitcast(FP8X4), va_plane[0][:], tok_a)
         sigmoid("a0", banks[0])
@@ -164,8 +164,10 @@ def tile_moe_experts_write_with_weights_kernel(
         product(banks[1], fp4_cols(wa_t, 0), wa_plane[:, cols(0)], tok_a)
         values("a0", banks[1])
         tok_b = gather_tokens("b", list_b)
-        quantise_va(1)
-        win["b1"] = tile("win_b1", [P, T], F32, tag="va_bf1")
+        quantise_va(1, nc.scalar.copy)
+        po0 = tile("po0", [P, T], F32)
+        nc.vector.tensor_tensor(po0[:], pr_t[0][:], old_t[0][:], ALU.mult)
+        win["b1"] = tile("win_b1", [P, T], F32, tag="old0")
         nc.gpsimd.memset(win["b1"][:], 0.0)
         softplus("a0", banks[0])
         win["b2"] = tile("win_b2", [P, T], F32, tag="lg_a0")
@@ -187,16 +189,14 @@ def tile_moe_experts_write_with_weights_kernel(
             values(key, banks[b])
         den = [[banks[2], banks[4]], banks[0:2]]
         num = [[banks[5], banks[3]], banks[6:8]]
-        po0 = pair["a0"]
-        nc.gpsimd.tensor_tensor(po0[:], pr_t[0][:], old_t[0][:], ALU.mult)
+        po1 = pair["a0"]
+        nc.gpsimd.tensor_tensor(po1[:], pr_t[1][:], old_t[1][:], ALU.mult)
         turn_add(den[0], pr_t[0], True, False)
         turn_add(den[0], win["a1"], False, False)
         softplus("a1", banks[0])
-        po1 = tile("po1", [P, T], F32, tag="lg_a1")
-        nc.gpsimd.tensor_tensor(po1[:], pr_t[1][:], old_t[1][:], ALU.mult)
         softplus("b0", banks[6])
-        scatter_weights("a1", "a1")
         softplus("b1", banks[3])
+        scatter_weights("a1", "a1")
         scatter_weights("b0", "b1")
         scatter_weights("b1", "b2")
         turn_add(den[1], pr_t[1], True, False)

from contextlib import ExitStack

import concourse.mybir as mybir
from concourse.masks import make_identity

K, T, J, N = 512, 1024, 512, 256
FLOPS = 4 * 2 * K * N * J

F32 = mybir.dt.float32
BF16 = mybir.dt.bfloat16
I32 = mybir.dt.int32
U32 = mybir.dt.uint32
U16 = mybir.dt.uint16
U8 = mybir.dt.uint8
FP8X4 = mybir.dt.float8_e4m3fn_x4
FP4X4 = mybir.dt.float4_e2m1fn_x4
ACT = mybir.ActivationFunctionType
ALU = mybir.AluOpType

P = 128
BANK = 512
TINY = 2.0 ** -60


def tile_moe_experts_write_with_weights_kernel(
    tc, xt_words, xt_scales, wa_words, wa_scales, va, wb_words, wb_scales, vb_words, vb_scales, pr, old, offs, offs2, out
):
    nc = tc.nc
    with ExitStack() as ctx:
        lists = ctx.enter_context(tc.tile_pool(name="lists", bufs=1))
        sb = ctx.enter_context(tc.tile_pool(name="sb", bufs=1))
        psum = ctx.enter_context(tc.psum_pool(name="psum", bufs=1))

        def tile(name, shape, dtype, tag=None):
            return sb.tile(shape, dtype, name=name, tag=tag or name, align_bytes=64)

        banks = [psum.tile([P, BANK], F32, name="bank%d" % i) for i in range(8)]

        list_a = lists.tile([P, J // 16], U16, name="list_a")
        list_b = lists.tile([P, J // 16], U16, name="list_b")
        x_words = tile("x_words", [P, T], I32)
        x_plane = tile("x_plane", [P, T], U8)
        w_planes = tile("w_planes", [P, 3 * N], U8)
        wa_plane, vb_plane, wb_plane = (w_planes[:, i * N : (i + 1) * N] for i in range(3))
        wa_t = tile("wa_t", [P, 2 * N], U8)
        wb_t = tile("wb_t", [P, 2 * N], U8)
        vb_t = tile("vb_t", [P, N], I32)
        va_raw = [tile("va_raw%d" % r, [P, 4, P], F32) for r in range(2)]
        pr_t = [tile("pr%d" % r, [P, T], F32) for r in range(2)]
        old_t = [tile("old%d" % r, [P, T], F32) for r in range(2)]
        win = {name: tile("win_" + name, [P, T], F32) for name in ("a1", "a2")}
        tiny = tile("tiny", [P, 1], F32)
        ident = tile("ident", [P, P], F32)

        def load_plane(queue, plane, scales):
            for s in range(4):
                queue.dma_start(out=plane[s:P:32, :].bitcast(I32), in_=scales[0][s:16:4, :].bitcast(I32))

        nc.gpsimd.memset(x_plane[:].bitcast(I32), 0)
        nc.gpsimd.memset(w_planes[:].bitcast(I32), 0)
        nc.gpsimd.memset(tiny[:], TINY)
        for name in ("a1", "a2"):
            nc.vector.memset(win[name][:], 0.0)
        make_identity(nc, ident[:])

        va_rows = va.rearrange("(p j) n -> p j n", j=4)
        nc.sync.dma_start(list_a[:], offs)
        nc.sync.dma_start(out=va_raw[0][:], in_=va_rows[:, :, 0:P])
        load_plane(nc.sync, x_plane, xt_scales)
        nc.sync.dma_start(out=x_words[:], in_=xt_words[0].rearrange("p n t -> p (n t)").bitcast(I32))
        nc.sync.dma_start(out=va_raw[1][:], in_=va_rows[:, :, P : 2 * P])
        nc.sync.dma_start(out=wa_t[:].bitcast(I32), in_=wa_words[0].bitcast(I32))
        nc.sync.dma_start(list_b[:], offs2)
        nc.sync.dma_start(out=pr_t[0][:], in_=pr[0:P, :])
        nc.sync.dma_start(out=old_t[0][:], in_=old[0:P, :])
        load_plane(nc.sync, wa_plane, wa_scales)
        nc.sync.dma_start(out=vb_t[:], in_=vb_words[0].rearrange("p n t -> p (n t)").bitcast(I32))
        load_plane(nc.sync, vb_plane, vb_scales)
        nc.sync.dma_start(out=wb_t[:].bitcast(I32), in_=wb_words[0].bitcast(I32))
        nc.sync.dma_start(out=pr_t[1][:], in_=pr[P : 2 * P, :])
        nc.sync.dma_start(out=old_t[1][:], in_=old[P : 2 * P, :])
        load_plane(nc.sync, wb_plane, wb_scales)

        va_codes = [tile("va_codes%d" % r, [P, P], U32) for r in range(2)]
        va_plane = [tile("va_plane%d" % r, [P, P], U8) for r in range(2)]

        def quantise_va(r, cast):
            grouped = tile("va_bf%d" % r, [P, P, 4], BF16)
            cast(
                out=grouped[:].rearrange("p (c i) t -> p c t i", i=4),
                in_=va_raw[r][:].rearrange("p t (c i) -> p c t i", i=4),
            )
            nc.vector.quantize_mx(
                out=va_codes[r][:].bitcast(FP8X4), scales=va_plane[r][:], in_=grouped[:].rearrange("p n t -> p (n t)")
            )

        def gather_tokens(name, lst):
            words = tile("g_words_" + name, [P, J], U32)
            plane = tile("g_plane_" + name, [P, J], U8)
            nc.vector.tensor_copy(plane[:], x_plane[:].indirect(lst[:]))
            nc.vector.tensor_copy(words[:], x_words[:].bitcast(U32).indirect(lst[:]))
            return words, plane

        def product(bank, lhs, lhs_plane, tokens):
            nc.tensor.matmul_mx(
                out=bank[:], lhsT=lhs, lhsT_scale=lhs_plane, rhs=tokens[0][:].bitcast(FP8X4), rhs_scale=tokens[1][:],
                start=True, stop=True,
            )

        def cols(r):
            return slice(r * P, (r + 1) * P)

        def fp4_cols(words, r):
            return words[:, 2 * r * P : 2 * (r + 1) * P].bitcast(FP4X4)

        keys = ("a0", "b0", "b1", "a1")
        pair = {key: tile("pair_" + key, [P, 2 * J], F32) for key in keys}
        wgt = {key: pair[key][:, 0:J] for key in keys}
        val = {key: pair[key][:, J : 2 * J] for key in keys}
        lg = {key: tile("lg_" + key, [P, J], F32) for key in keys}
        lists_of = {"a": list_a, "b": list_b}

        def sigmoid(key, bank):
            nc.scalar.activation(val[key], bank[:], ACT.Sigmoid, scale=-1.0)

        def logarithm(key):
            nc.scalar.activation(lg[key][:], val[key], ACT.Ln, bias=tiny[:])

        def softplus(key, bank):
            nc.vector.scalar_tensor_tensor(wgt[key], lg[key][:], -1.0, bank[:], ALU.mult, ALU.max)

        def values(key, bank):
            nc.scalar.copy(val[key], bank[:])

        def scatter_weights(key, window):
            nc.vector.tensor_copy(win[window][:].indirect(lists_of[key[0]][:]), wgt[key])

        def scatter_products(key, window):
            nc.vector.tensor_tensor(win[window][:].indirect(lists_of[key[0]][:]), wgt[key], val[key], ALU.mult)

        def turn_add(two_banks, src, first, last):
            for h in range(2):
                for c in range(4):
                    nc.tensor.matmul(
                        two_banks[h][:, cols(c)], lhsT=src[:, cols(4 * h + c)], rhs=ident[:], is_transpose=True,
                        start=(first and c == 0), stop=(last and c == 3),
                    )

        def turn_back(name, two_banks, func):
            for h in range(2):
                mid = tile("mid_%s%d" % (name, h), [P, BANK], F32)
                nc.scalar.activation(mid[:], two_banks[h][:], func)
                for c in range(4):
                    nc.tensor.transpose(two_banks[h][:, cols(c)], mid[:, cols(c)], ident[:])

        def half(h):
            return slice(h * BANK, (h + 1) * BANK)

        quantise_va(0, nc.vector.tensor_copy)
        tok_a = gather_tokens("a", list_a)
        product(banks[0], va_codes[0][:].bitcast(FP8X4), va_plane[0][:], tok_a)
        sigmoid("a0", banks[0])
        logarithm("a0")
        product(banks[1], fp4_cols(wa_t, 0), wa_plane[:, cols(0)], tok_a)
        values("a0", banks[1])
        tok_b = gather_tokens("b", list_b)
        quantise_va(1, nc.scalar.copy)
        po0 = tile("po0", [P, T], F32)
        nc.vector.tensor_tensor(po0[:], pr_t[0][:], old_t[0][:], ALU.mult)
        win["b1"] = tile("win_b1", [P, T], F32, tag="old0")
        nc.gpsimd.memset(win["b1"][:], 0.0)
        softplus("a0", banks[0])
        win["b2"] = tile("win_b2", [P, T], F32, tag="lg_a0")
        nc.gpsimd.memset(win["b2"][:], 0.0)
        scatter_weights("a0", "a1")
        scatter_products("a0", "a2")

        product(banks[0], va_codes[1][:].bitcast(FP8X4), va_plane[1][:], tok_a)
        product(banks[6], vb_t[:, cols(0)].bitcast(FP8X4), vb_plane[:, cols(0)], tok_b)
        product(banks[3], vb_t[:, cols(1)].bitcast(FP8X4), vb_plane[:, cols(1)], tok_b)
        product(banks[1], fp4_cols(wa_t, 1), wa_plane[:, cols(1)], tok_a)
        product(banks[5], fp4_cols(wb_t, 0), wb_plane[:, cols(0)], tok_b)
        product(banks[7], fp4_cols(wb_t, 1), wb_plane[:, cols(1)], tok_b)
        for key, b in (("a1", 0), ("b0", 6), ("b1", 3)):
            sigmoid(key, banks[b])
        for key in ("a1", "b0", "b1"):
            logarithm(key)
        for key, b in (("b0", 5), ("a1", 1), ("b1", 7)):
            values(key, banks[b])
        den = [[banks[2], banks[4]], banks[0:2]]
        num = [[banks[5], banks[3]], banks[6:8]]
        po1 = pair["a0"]
        nc.gpsimd.tensor_tensor(po1[:], pr_t[1][:], old_t[1][:], ALU.mult)
        turn_add(den[0], pr_t[0], True, False)
        turn_add(den[0], win["a1"], False, False)
        softplus("a1", banks[0])
        softplus("b0", banks[6])
        softplus("b1", banks[3])
        scatter_weights("a1", "a1")
        scatter_weights("b0", "b1")
        scatter_weights("b1", "b2")
        turn_add(den[1], pr_t[1], True, False)
        turn_add(den[1], win["a1"], False, False)
        turn_add(num[0], win["a2"], True, False)
        turn_add(num[0], po0, False, False)
        turn_add(num[1], po1, True, False)
        turn_add(den[0], win["b1"], False, True)
        ln_den0 = tile("ln_den0", [P, T], F32)
        for h in range(2):
            nc.scalar.activation(ln_den0[:, half(h)], den[0][h][:], ACT.Ln)
        scatter_products("a1", "a2")
        turn_add(den[1], win["b2"], False, True)
        ln_den1 = tile("ln_den1", [P, T], F32)
        rec0 = tile("rec0", [P, T], F32)
        rec1_turned = tile("rec1_turned", [P, T], F32)
        for h in range(2):
            nc.scalar.activation(ln_den1[:, half(h)], den[1][h][:], ACT.Ln)
        for h in range(2):
            for c in range(4):
                nc.tensor.transpose(den[1][h][:, cols(c)], ln_den0[:, cols(4 * h + c)], ident[:])
            nc.scalar.activation(rec0[:, half(h)], den[1][h][:], ACT.Exp, scale=-1.0)
        for h in range(2):
            nc.scalar.activation(rec1_turned[:, half(h)], ln_den1[:, half(h)], ACT.Exp, scale=-1.0)
        scatter_products("b0", "b1")
        turn_add(num[1], win["a2"], False, True)
        turn_back("num1", num[1], ACT.Copy)
        scatter_products("b1", "b2")
        turn_add(num[0], win["b1"], False, True)
        turn_back("num0", num[0], ACT.Copy)
        y = [tile("y%d" % r, [P, T], F32) for r in range(2)]
        num0 = tile("num0", [P, T], F32)
        for h in range(2):
            nc.scalar.copy(num0[:, half(h)], num[0][h][:])
            nc.gpsimd.tensor_tensor(y[0][:, half(h)], num0[:, half(h)], rec0[:, half(h)], ALU.mult)
        rec1 = num[0]
        for h in range(2):
            for c in range(4):
                nc.tensor.transpose(rec1[h][:, cols(c)], rec1_turned[:, cols(4 * h + c)], ident[:])
        total = tile("total", [P, T], F32)
        for h in range(2):
            nc.vector.tensor_tensor(total[:, half(h)], num[1][h][:], win["b2"][:, half(h)], ALU.add)
        for h in range(2):
            nc.vector.tensor_tensor(y[1][:, half(h)], rec1[h][:], total[:, half(h)], ALU.mult)
        for h in range(2):
            for r in range(2):
                nc.sync.dma_start(out=out[r * P : (r + 1) * P, half(h)], in_=y[r][:, half(h)])
